import numpy as np
import ml_dtypes


def mxq(x, axis, fmt="e4m3"):
    dtype, down = {"e4m3": (ml_dtypes.float8_e4m3fn, 7), "e5m2": (ml_dtypes.float8_e5m2, 14)}[fmt]
    v = np.moveaxis(np.asarray(x, np.float32).astype(ml_dtypes.bfloat16).astype(np.float64), axis, -1)
    blocks = v.reshape(v.shape[:-1] + (-1, 32))
    amax = np.abs(blocks).max(-1, keepdims=True)
    byte = np.maximum(np.where(amax > 0, np.frexp(amax)[1] - 1 + 127, 0) - down, 1)
    scale = np.exp2(byte - 127.0)
    codes = (blocks / scale).astype(np.float32).astype(dtype).astype(np.float64)
    return np.moveaxis((codes * scale).reshape(v.shape), -1, axis)


WIDE = False


def mx_kscale(k):
    if not WIDE:
        return np.ones(k)
    levels = np.array([10, -10, 5, -5, 0])
    if k % 512:
        return np.exp2(np.random.permutation(np.resize(levels, k // 32))).repeat(32)
    a = np.empty((k // 512, 16))
    for p in range(k // 512):
        a[p, :8] = np.random.permutation(np.resize(levels, 8))
        for g in range(8):
            far = levels[np.abs(levels - a[p, g]) >= 10]
            a[p, g + 8] = far[np.random.randint(len(far))]
    return np.exp2(a.ravel()).repeat(32)


def f64(x):
    return np.asarray(x).astype(np.float64)


def striped(idx):
    return np.tile(np.asarray(idx).reshape(-1, 16).T, (8, 1)).astype(np.uint16)


def unstriped(offs):
    return offs[:16].T.reshape(-1).astype(np.int64)


def striped8(idx):
    return np.asarray(idx).reshape(8, -1, 16).transpose(0, 2, 1).reshape(128, -1).astype(np.uint16)


def unstriped8(offs):
    return offs.reshape(8, 16, -1).transpose(0, 2, 1).reshape(8, -1).astype(np.int64)


def pick8(x, idx, run):
    r = np.arange(len(x))
    return x[r[:, None], idx[r % (8 * run) // run]]


E2M1 = np.array([0.0, 0.5, 1.0, 1.5, 2.0, 3.0, 4.0, 6.0, -0.0, -0.5, -1.0, -1.5, -2.0, -3.0, -4.0, -6.0])


def pack_weight(w, fmt):
    k, n = w.shape
    w = f64(np.asarray(w, np.float32).astype(ml_dtypes.bfloat16)).reshape(k // 32, 32, n)
    amax = np.abs(w).max(1)
    if fmt == "e4m3":
        byte = np.frexp(amax)[1] - 1 + 127 - 7
    else:
        mant, ex = np.frexp(amax / 6.0)
        byte = np.where(mant > 0.5, ex, ex - 1) + 127
    byte = np.clip(np.where(amax > 0, byte, 1), 1, 254)
    scaled = (w * np.exp2(127.0 - byte)[:, None, :]).reshape(k, n).astype(np.float32)
    by_word = np.ascontiguousarray(scaled.reshape(k // 512, 128, 4, n).transpose(0, 1, 3, 2))
    if fmt == "e4m3":
        words = by_word.astype(ml_dtypes.float8_e4m3fn).view(np.uint8)
    else:
        c = by_word.astype(ml_dtypes.float4_e2m1fn).view(np.uint8) & 0xF
        words = (c[..., 0::2] | (c[..., 1::2] << 4)).reshape(k // 512, 128, 2 * n)
    return np.ascontiguousarray(words), np.ascontiguousarray(byte.astype(np.uint8).reshape(k // 512, 16, n))


def unpack_weight(words, scales, fmt):
    g, _, n = scales.shape
    words = np.ascontiguousarray(words).reshape(g, 128, n, -1)
    if fmt == "e4m3":
        vals = words.view(ml_dtypes.float8_e4m3fn).astype(np.float64)
    else:
        nib = np.empty((g, 128, n, 4), np.uint8)
        nib[..., 0::2] = words & 0xF
        nib[..., 1::2] = words >> 4
        vals = E2M1[nib]
    vals = vals * np.repeat(np.exp2(scales.astype(np.float64) - 127.0), 8, axis=1)[..., None]
    return vals.transpose(0, 1, 3, 2).reshape(g * 512, n)


K, J, R, T, U, Z, M, O, C, N, S, V = 512, 256, 512, 1024, 1024, 512, 1024, 128, 512, 256, 512, 1024


def setup_inputs():
    n = np.random.standard_normal
    idx = np.stack([np.random.permutation(T)[:J] for _ in range(8)])
    idx2 = np.stack([np.random.permutation(U)[:J] for _ in range(8)])
    idx3 = np.random.permutation(M)[:J]
    idx4 = np.stack([np.random.permutation(C)[:J] for _ in range(8)])
    idx5 = np.stack([np.random.permutation(C)[:J] for _ in range(8)])
    idx6 = np.stack([np.random.permutation(J)[:O] for _ in range(8)])
    idx7 = np.random.permutation(V)[:O]
    fk = mx_kscale(K)
    fr = mx_kscale(R)
    fz = mx_kscale(Z)
    fs = mx_kscale(S)
    wp = pack_weight(n((K, R)) * 1 / np.sqrt(K) / fk[:, None] * fr, "e2m1")
    xop = pack_weight(n((Z, M)) / fz[:, None], "e2m1")
    w2p = pack_weight(n((Z, R)) * 1 / np.sqrt(Z) * fz[:, None] * fr, "e4m3")
    wbp = pack_weight(n((R, N)) * 1 / np.sqrt(R) / fr[:, None], "e4m3")
    xrp = pack_weight(n((S, V)) / fs[:, None], "e2m1")
    wsp = pack_weight(n((S, N)) * 1 / np.sqrt(S) * fs[:, None], "e4m3")
    return {
        "ta": (np.random.randint(-7, 8, (K, T)).astype(np.float64)).astype(np.float32),
        "tb": (np.random.randint(1, 9, (K, U)).astype(np.float64)).astype(np.float32),
        "ga": ((np.random.randint(8, 25, (K, 1)) / 64.0) * fk[:, None]).astype(np.float32),
        "gb": (np.random.uniform(0.1, 0.4, (K, 1))).astype(np.float32),
        "w_words": wp[0],
        "w_scales": wp[1],
        "xo_words": xop[0],
        "xo_scales": xop[1],
        "w2_words": w2p[0],
        "w2_scales": w2p[1],
        "sa": (np.random.uniform(0.5, 1.6, (R, 1))).astype(np.float32),
        "sb": (np.random.uniform(0.5, 1.6, (R, 1))).astype(np.float32),
        "wb_words": wbp[0],
        "wb_scales": wbp[1],
        "xr_words": xrp[0],
        "xr_scales": xrp[1],
        "ws_words": wsp[0],
        "ws_scales": wsp[1],
        "offs": striped8(idx),
        "offs2": striped8(idx2),
        "offs3": striped(idx3),
        "offs4": striped8(idx4),
        "offs5": striped8(idx5),
        "offs6": striped8(idx6),
        "offs7": striped(idx7),
    }


def reference(ta, tb, ga, gb, w_words, w_scales, xo_words, xo_scales, w2_words, w2_scales, sa, sb, wb_words, wb_scales, xr_words, xr_scales, ws_words, ws_scales, offs, offs2, offs3, offs4, offs5, offs6, offs7):
    idx = unstriped8(offs)
    idx2 = unstriped8(offs2)
    idx3 = unstriped(offs3)
    idx4 = unstriped8(offs4)
    idx5 = unstriped8(offs5)
    idx6 = unstriped8(offs6)
    idx7 = unstriped(offs7)
    wu = unpack_weight(w_words, w_scales, "e2m1")
    xou = unpack_weight(xo_words, xo_scales, "e2m1")
    w2u = unpack_weight(w2_words, w2_scales, "e4m3")
    wbu = unpack_weight(wb_words, wb_scales, "e4m3")
    xru = unpack_weight(xr_words, xr_scales, "e2m1")
    wsu = unpack_weight(ws_words, ws_scales, "e4m3")
    xc = pick8(f64(ta), idx, 64) * f64(ga) * pick8(f64(tb), idx2, 64) * f64(gb)
    xcq = mxq(xc, 0, "e4m3")
    a = wu.T @ xcq
    xoidx3g = xou[:, idx3]
    b = w2u.T @ xoidx3g
    pw = np.zeros((R, C))
    pw[np.arange(R)[:, None], idx4[np.arange(R) % 512 // 64]] = a
    g1 = np.maximum(pick8(pw, idx5, 64) * f64(sa), b)
    hid = pick8(g1, idx6, 64) * f64(sb)
    hidq = mxq(hid, 0, "e4m3")
    xridx7g = xru[:, idx7]
    y = wbu.T @ hidq + wsu.T @ xridx7g
    return y

@@ -1,0 +1,238 @@
+from contextlib import ExitStack
+
+import concourse.mybir as mybir
+
+K, J, R, T, M, O, C, N, V = 512, 256, 512, 1024, 1024, 128, 512, 256, 1024
+FLOPS = 2 * (K * R * J + 512 * R * J + R * N * O + 512 * N * O)
+
+F32 = mybir.dt.float32
+BF16 = mybir.dt.bfloat16
+I32 = mybir.dt.int32
+U32 = mybir.dt.uint32
+U16 = mybir.dt.uint16
+U8 = mybir.dt.uint8
+FP8X4 = mybir.dt.float8_e4m3fn_x4
+FP4X4 = mybir.dt.float4_e2m1fn_x4
+COPY = mybir.ActivationFunctionType.Copy
+MULT = mybir.AluOpType.mult
+MAX = mybir.AluOpType.max
+
+P = 128
+PACK = 4
+HALF = J // 2
+
+
+def tile_picked_codegain_plain_two_answered_reminder_plain_kernel(
+    tc, ta, tb, ga, gb, w_words, w_scales, xo_words, xo_scales, w2_words, w2_scales, sa, sb,
+    wb_words, wb_scales, xr_words, xr_scales, ws_words, ws_scales,
+    offs, offs2, offs3, offs4, offs5, offs6, offs7, out,
+):
+    nc = tc.nc
+    with ExitStack() as ctx:
+        keep = ctx.enter_context(tc.tile_pool(name="keep", bufs=1))
+        psum = ctx.enter_context(tc.psum_pool(name="psum", bufs=1))
+
+        def sb_tile(name, shape, dtype, tag=None):
+            return keep.tile(shape, dtype, name=name, tag=tag or name, align_bytes=64)
+
+        def load_list(name, src):
+            lst = keep.tile(list(src.shape), U16, name=name)
+            nc.sync.dma_start(lst[:], src)
+            return lst
+
+        def load_gain(name, src):
+            gain = keep.tile([P, PACK], F32, name=name)
+            nc.sync.dma_start(gain[:], src.rearrange("(p t) o -> p (t o)", t=PACK))
+            return gain
+
+        def load_rows(name, src, t):
+            rows = sb_tile(name, [P, T], F32)
+            nc.sync.dma_start(rows[:], src.rearrange("(p t) c -> p t c", t=PACK)[:, t, :])
+            return rows
+
+        def zeroed_plane(name, width):
+            plane = sb_tile(name, [P, width], U8)
+            nc.vector.memset(plane[:].bitcast(I32), 0)
+            return plane
+
+        def load_plane(plane, src, rows=range(4)):
+            by_row = src[0].rearrange("(q r) n -> r q n", r=4)
+            for r in rows:
+                nc.sync.dma_start(plane[r:P:32, :].bitcast(I32), by_row[r].bitcast(I32))
+
+        def load_fp4_words(name, src, width):
+            words = sb_tile(name, [P, width], U16)
+            nc.sync.dma_start(words[:].bitcast(I32), src[0].bitcast(I32))
+            return words
+
+        def load_fp8_words(name, src, width):
+            words = sb_tile(name, [P, width], U32)
+            nc.sync.dma_start(words[:].bitcast(I32), src[0].rearrange("p n t -> p (n t)").bitcast(I32))
+            return words
+
+        def dealt(src):
+            return src[:].rearrange("p (m t) -> p t m", t=PACK)
+
+        w_plane_raw = zeroed_plane("w_plane_raw", R)
+        xo_plane_all = zeroed_plane("xo_plane_all", M)
+        w2_plane_raw = zeroed_plane("w2_plane_raw", R)
+        xr_plane_all = zeroed_plane("xr_plane_all", V)
+        ws_plane = zeroed_plane("ws_plane", N)
+        wb_plane = zeroed_plane("wb_plane", N)
+        board = []
+        for t in range(PACK):
+            board.append(sb_tile("board%d" % t, [P, C], F32))
+            nc.vector.memset(board[t][:], 0.0)
+
+        ta_rows, tb_rows = [], []
+        ta_rows.append(load_rows("ta0", ta, 0))
+        l1 = load_list("l1", offs)
+        ga_t = load_gain("ga_t", ga)
+        tb_rows.append(load_rows("tb0", tb, 0))
+        l2 = load_list("l2", offs2)
+        gb_t = load_gain("gb_t", gb)
+        load_plane(w_plane_raw, w_scales, [0])
+        ta_rows.append(load_rows("ta1", ta, 1))
+        load_plane(w_plane_raw, w_scales, [1, 2])
+        tb_rows.append(load_rows("tb1", tb, 1))
+        load_plane(w_plane_raw, w_scales, [3])
+        load_plane(xo_plane_all, xo_scales, [0, 1])
+        ta_rows.append(load_rows("ta2", ta, 2))
+        load_plane(xo_plane_all, xo_scales, [2, 3])
+        tb_rows.append(load_rows("tb2", tb, 2))
+        l3 = load_list("l3", offs3)
+        load_plane(w2_plane_raw, w2_scales, [0, 1])
+        ta_rows.append(load_rows("ta3", ta, 3))
+        load_plane(w2_plane_raw, w2_scales, [2, 3])
+        tb_rows.append(load_rows("tb3", tb, 3))
+        w_raw = load_fp4_words("w_raw", w_words, R)
+        xo_all = load_fp4_words("xo_all", xo_words, M)
+        l4 = load_list("l4", offs4)
+        w2_raw = load_fp8_words("w2_raw", w2_words, R)
+        l5 = load_list("l5", offs5)
+        sa_t = load_gain("sa_t", sa)
+        l6 = load_list("l6", offs6)
+        sb_t = load_gain("sb_t", sb)
+        l7 = load_list("l7", offs7)
+        load_plane(xr_plane_all, xr_scales)
+        xr_all = load_fp4_words("xr_all", xr_words, V)
+        ws_codes = load_fp8_words("ws_codes", ws_words, N)
+        load_plane(ws_plane, ws_scales)
+        wb_codes = load_fp8_words("wb_codes", wb_words, N)
+        load_plane(wb_plane, wb_scales)
+
+        xc = [sb_tile("xc%d" % h, [P, HALF, PACK], BF16) for h in range(2)]
+        w_plane = sb_tile("w_plane", [P, PACK, P], U8)
+        xo_plane = sb_tile("xo_plane", [P, J], U8)
+        w2_plane = sb_tile("w2_plane", [P, PACK, P], U8)
+        for t in range(PACK):
+            step = sb_tile("step%d" % t, [P, J], F32)
+            gain = sb_tile("gain%d" % t, [P, J], F32)
+            nc.scalar.activation(out=step[:], in_=ta_rows[t][:].indirect(l1[:]), func=COPY, scale=ga_t[:, t : t + 1])
+            nc.scalar.activation(out=gain[:], in_=tb_rows[t][:].indirect(l2[:]), func=COPY, scale=gb_t[:, t : t + 1])
+            for h in range(2):
+                cols = slice(h * HALF, (h + 1) * HALF)
+                nc.vector.tensor_tensor(out=xc[h][:, :, t], in0=step[:, cols], in1=gain[:, cols], op=MULT)
+            if t == 1:
+                nc.vector.tensor_copy(out=w_plane[:], in_=dealt(w_plane_raw))
+            if t == 2:
+                nc.vector.tensor_copy(out=xo_plane[:], in_=xo_plane_all[:].indirect(l3[:]))
+                nc.vector.tensor_copy(out=w2_plane[:], in_=dealt(w2_plane_raw))
+
+        w_codes = sb_tile("w_codes", [P, PACK, P], U16)
+        for t in range(PACK):
+            nc.scalar.copy(out=w_codes[:, t, :], in_=dealt(w_raw)[:, t, :])
+
+        xc_codes = sb_tile("xc_codes", [P, J], U32)
+        xc_plane = sb_tile("xc_plane", [P, J], U8)
+        for h in range(2):
+            cols = slice(h * HALF, (h + 1) * HALF)
+            nc.vector.quantize_mx(
+                out=xc_codes[:, cols].bitcast(FP8X4), scales=xc_plane[:, cols],
+                in_=xc[h][:].rearrange("p j t -> p (j t)"),
+            )
+
+        a_sb = sb_tile("a_sb", [P, PACK, J], F32)
+        bank_a0 = psum.tile([P, HALF], F32, name="bank_a0")
+        bank_a1 = psum.tile([P, HALF], F32, name="bank_a1")
+        bank_a2 = psum.tile([P, J], F32, name="bank_a2")
+        bank_a3 = psum.tile([P, 2, J], F32, name="bank_a3")
+
+        def first_product(dst, t, cols):
+            nc.tensor.matmul_mx(
+                out=dst, lhsT=w_codes[:, t, :].bitcast(FP4X4), lhsT_scale=w_plane[:, t, :],
+                rhs=xc_codes[:, cols].bitcast(FP8X4), rhs_scale=xc_plane[:, cols], start=True, stop=True,
+            )
+
+        first_product(bank_a0[:], 0, slice(0, HALF))
+        first_product(bank_a1[:], 0, slice(HALF, J))
+        first_product(bank_a2[:], 1, slice(0, J))
+        first_product(bank_a3[:, 0, :], 2, slice(0, J))
+        first_product(bank_a3[:, 1, :], 3, slice(0, J))
+        nc.scalar.copy(out=a_sb[:, 0, 0:HALF], in_=bank_a0[:])
+        nc.scalar.copy(out=a_sb[:, 0, HALF:J], in_=bank_a1[:])
+        nc.scalar.copy(out=a_sb[:, 1, :], in_=bank_a2[:])
+        nc.scalar.copy(out=a_sb[:, 2:4, :], in_=bank_a3[:])
+
+        xo_codes = sb_tile("xo_codes", [P, J], U16, tag="xc1")
+        nc.vector.tensor_copy(out=xo_codes[:], in_=xo_all[:].indirect(l3[:]))
+
+        for h in range(2):
+            nc.vector.tensor_copy(
+                out=board[0][:].indirect(l4[:, h * 8 : (h + 1) * 8]), in_=a_sb[:, 0, h * HALF : (h + 1) * HALF]
+            )
+        for t in range(1, PACK):
+            nc.vector.tensor_copy(out=board[t][:].indirect(l4[:]), in_=a_sb[:, t, :])
+
+        w2_codes = sb_tile("w2_codes", [P, PACK, P], U32)
+        nc.scalar.copy(out=w2_codes[:], in_=dealt(w2_raw))
+        bank_b = [psum.tile([P, 2, J], F32, name="bank_b%d" % u) for u in range(2)]
+        for t in range(PACK):
+            nc.tensor.matmul_mx(
+                out=bank_b[t // 2][:, t % 2, :], lhsT=w2_codes[:, t, :].bitcast(FP8X4), lhsT_scale=w2_plane[:, t, :],
+                rhs=xo_codes[:].bitcast(FP4X4), rhs_scale=xo_plane[:], start=True, stop=True,
+            )
+
+        read = []
+        for t in range(PACK):
+            read.append(sb_tile("read%d" % t, [P, J], F32, tag="w2_raw" if t == 0 else None))
+            nc.scalar.activation(out=read[t][:], in_=board[t][:].indirect(l5[:]), func=COPY, scale=sa_t[:, t : t + 1])
+        answer = []
+        for t in range(PACK):
+            answer.append(sb_tile("answer%d" % t, [P, J], F32))
+            nc.vector.tensor_tensor(out=answer[t][:], in0=read[t][:], in1=bank_b[t // 2][:, t % 2, :], op=MAX)
+        hid_rows = sb_tile("hid_rows", [P, PACK, O], BF16)
+        for t in range(PACK):
+            nc.scalar.activation(out=hid_rows[:, t, :], in_=answer[t][:].indirect(l6[:]), func=COPY, scale=sb_t[:, t : t + 1])
+
+        xr_plane = sb_tile("xr_plane", [P, O], U8, tag="read3")
+        xr_codes = sb_tile("xr_codes", [P, O], U16, tag="read2")
+        nc.vector.tensor_copy(out=xr_plane[:], in_=xr_plane_all[:].indirect(l7[:]))
+        nc.vector.tensor_copy(out=xr_codes[:], in_=xr_all[:].indirect(l7[:]))
+        bank_y = [psum.tile([P, O], F32, name="bank_y%d" % u) for u in range(2)]
+        for u in range(2):
+            cols = slice(u * P, (u + 1) * P)
+            nc.tensor.matmul_mx(
+                out=bank_y[u][:], lhsT=ws_codes[:, cols].bitcast(FP8X4), lhsT_scale=ws_plane[:, cols],
+                rhs=xr_codes[:].bitcast(FP4X4), rhs_scale=xr_plane[:], start=True, stop=False,
+            )
+
+        hid = sb_tile("hid", [P, O, PACK], BF16, tag="xr_all")
+        nc.vector.tensor_copy(out=hid[:], in_=hid_rows[:].rearrange("p t o -> p o t"))
+        hid_codes = sb_tile("hid_codes", [P, O], U32)
+        hid_plane = sb_tile("hid_plane", [P, O], U8)
+        nc.vector.quantize_mx(
+            out=hid_codes[:].bitcast(FP8X4), scales=hid_plane[:], in_=hid[:].rearrange("p o t -> p (o t)")
+        )
+        for u in range(2):
+            cols = slice(u * P, (u + 1) * P)
+            nc.tensor.matmul_mx(
+                out=bank_y[u][:], lhsT=wb_codes[:, cols].bitcast(FP8X4), lhsT_scale=wb_plane[:, cols],
+                rhs=hid_codes[:].bitcast(FP8X4), rhs_scale=hid_plane[:], start=False, stop=True,
+            )
+        y0 = sb_tile("y0", [P, O], F32)
+        y1 = sb_tile("y1", [P, O], F32)
+        nc.vector.tensor_copy(out=y0[:], in_=bank_y[0][:])
+        nc.sync.dma_start(out[0:P, :], y0[:])
+        nc.scalar.copy(out=y1[:], in_=bank_y[1][:])
+        nc.scalar.dma_start(out[P:N, :], y1[:])

@@ -1,6 +1,7 @@
 from contextlib import ExitStack
 
 import concourse.mybir as mybir
+from concourse.masks import make_identity
 
 K, J, R, T, M, O, C, N, V = 512, 256, 512, 1024, 1024, 128, 512, 256, 1024
 FLOPS = 2 * (K * R * J + 512 * R * J + R * N * O + 512 * N * O)
@@ -30,6 +31,7 @@ def tile_picked_codegain_plain_two_answered_reminder_plain_kernel(
     nc = tc.nc
     with ExitStack() as ctx:
         keep = ctx.enter_context(tc.tile_pool(name="keep", bufs=1))
+        shared = ctx.enter_context(tc.tile_pool(name="shared", bufs=1))
         psum = ctx.enter_context(tc.psum_pool(name="psum", bufs=1))
 
         def sb_tile(name, shape, dtype, tag=None):
@@ -55,10 +57,26 @@ def tile_picked_codegain_plain_two_answered_reminder_plain_kernel(
             nc.vector.memset(plane[:].bitcast(I32), 0)
             return plane
 
-        def load_plane(plane, src, rows=range(4)):
+        def load_plane(plane, src):
             by_row = src[0].rearrange("(q r) n -> r q n", r=4)
-            for r in rows:
+            for r in range(4):
                 nc.sync.dma_start(plane[r:P:32, :].bitcast(I32), by_row[r].bitcast(I32))
+
+        def load_stage(name, src):
+            stage = sb_tile(name, [P, 2, src.shape[2]], U8)
+            by_row = src[0].rearrange("(q r) n -> r q n", r=4)
+            for u in range(2):
+                nc.sync.dma_start(
+                    stage[64 * u : 64 * u + 4, :, :].bitcast(I32), by_row[:, 2 * u : 2 * u + 2, :].bitcast(I32)
+                )
+            return stage
+
+        def spread_plane(plane, stage):
+            for q in range(4):
+                first = 64 * (q // 2)
+                nc.vector.tensor_copy(
+                    out=plane[32 * q : 32 * q + 4, :].bitcast(I32), in_=stage[first : first + 4, q % 2, :].bitcast(I32)
+                )
 
         def load_fp4_words(name, src, width):
             words = sb_tile(name, [P, width], U16)
@@ -75,7 +93,7 @@ def tile_picked_codegain_plain_two_answered_reminder_plain_kernel(
 
         w_plane_raw = zeroed_plane("w_plane_raw", R)
         xo_plane_all = zeroed_plane("xo_plane_all", M)
-        w2_plane_raw = zeroed_plane("w2_plane_raw", R)
+        w2_plane = zeroed_plane("w2_plane", R)
         xr_plane_all = zeroed_plane("xr_plane_all", V)
         ws_plane = zeroed_plane("ws_plane", N)
         wb_plane = zeroed_plane("wb_plane", N)
@@ -84,6 +102,9 @@ def tile_picked_codegain_plain_two_answered_reminder_plain_kernel(
             board.append(sb_tile("board%d" % t, [P, C], F32))
             nc.vector.memset(board[t][:], 0.0)
 
+        identity = sb_tile("identity", [P, P], F32)
+        make_identity(nc, identity[:])
+
         ta_rows, tb_rows = [], []
         ta_rows.append(load_rows("ta0", ta, 0))
         l1 = load_list("l1", offs)
@@ -91,24 +112,20 @@ def tile_picked_codegain_plain_two_answered_reminder_plain_kernel(
         tb_rows.append(load_rows("tb0", tb, 0))
         l2 = load_list("l2", offs2)
         gb_t = load_gain("gb_t", gb)
-        load_plane(w_plane_raw, w_scales, [0])
         ta_rows.append(load_rows("ta1", ta, 1))
-        load_plane(w_plane_raw, w_scales, [1, 2])
+        xo_stage = load_stage("xo_stage", xo_scales)
         tb_rows.append(load_rows("tb1", tb, 1))
-        load_plane(w_plane_raw, w_scales, [3])
-        load_plane(xo_plane_all, xo_scales, [0, 1])
+        w_stage = load_stage("w_stage", w_scales)
         ta_rows.append(load_rows("ta2", ta, 2))
-        load_plane(xo_plane_all, xo_scales, [2, 3])
-        tb_rows.append(load_rows("tb2", tb, 2))
         l3 = load_list("l3", offs3)
-        load_plane(w2_plane_raw, w2_scales, [0, 1])
+        tb_rows.append(load_rows("tb2", tb, 2))
         ta_rows.append(load_rows("ta3", ta, 3))
-        load_plane(w2_plane_raw, w2_scales, [2, 3])
         tb_rows.append(load_rows("tb3", tb, 3))
         w_raw = load_fp4_words("w_raw", w_words, R)
         xo_all = load_fp4_words("xo_all", xo_words, M)
         l4 = load_list("l4", offs4)
-        w2_raw = load_fp8_words("w2_raw", w2_words, R)
+        w2_codes = load_fp8_words("w2_codes", w2_words, R)
+        load_plane(w2_plane, w2_scales)
         l5 = load_list("l5", offs5)
         sa_t = load_gain("sa_t", sa)
         l6 = load_list("l6", offs6)
@@ -121,10 +138,14 @@ def tile_picked_codegain_plain_two_answered_reminder_plain_kernel(
         wb_codes = load_fp8_words("wb_codes", wb_words, N)
         load_plane(wb_plane, wb_scales)
 
-        xc = [sb_tile("xc%d" % h, [P, HALF, PACK], BF16) for h in range(2)]
+        spread_plane(xo_plane_all, xo_stage)
+        spread_plane(w_plane_raw, w_stage)
         w_plane = sb_tile("w_plane", [P, PACK, P], U8)
+        nc.vector.tensor_copy(out=w_plane[:], in_=dealt(w_plane_raw))
         xo_plane = sb_tile("xo_plane", [P, J], U8)
-        w2_plane = sb_tile("w2_plane", [P, PACK, P], U8)
+        nc.vector.tensor_copy(out=xo_plane[:], in_=xo_plane_all[:].indirect(l3[:]))
+
+        xc = [sb_tile("xc%d" % h, [P, HALF, PACK], BF16) for h in range(2)]
         for t in range(PACK):
             step = sb_tile("step%d" % t, [P, J], F32)
             gain = sb_tile("gain%d" % t, [P, J], F32)
@@ -133,11 +154,6 @@ def tile_picked_codegain_plain_two_answered_reminder_plain_kernel(
             for h in range(2):
                 cols = slice(h * HALF, (h + 1) * HALF)
                 nc.vector.tensor_tensor(out=xc[h][:, :, t], in0=step[:, cols], in1=gain[:, cols], op=MULT)
-            if t == 1:
-                nc.vector.tensor_copy(out=w_plane[:], in_=dealt(w_plane_raw))
-            if t == 2:
-                nc.vector.tensor_copy(out=xo_plane[:], in_=xo_plane_all[:].indirect(l3[:]))
-                nc.vector.tensor_copy(out=w2_plane[:], in_=dealt(w2_plane_raw))
 
         w_codes = sb_tile("w_codes", [P, PACK, P], U16)
         for t in range(PACK):
@@ -152,10 +168,10 @@ def tile_picked_codegain_plain_two_answered_reminder_plain_kernel(
                 in_=xc[h][:].rearrange("p j t -> p (j t)"),
             )
 
-        a_sb = sb_tile("a_sb", [P, PACK, J], F32)
+        a_all = shared.tile([P, PACK, J], F32, name="a_all", offset=0)
         bank_a0 = psum.tile([P, HALF], F32, name="bank_a0")
         bank_a1 = psum.tile([P, HALF], F32, name="bank_a1")
-        bank_a2 = psum.tile([P, J], F32, name="bank_a2")
+        bank_a2 = psum.tile([P, 2, HALF], F32, name="bank_a2")
         bank_a3 = psum.tile([P, 2, J], F32, name="bank_a3")
 
         def first_product(dst, t, cols):
@@ -165,47 +181,53 @@ def tile_picked_codegain_plain_two_answered_reminder_plain_kernel(
             )
 
         first_product(bank_a0[:], 0, slice(0, HALF))
-        first_product(bank_a1[:], 0, slice(HALF, J))
-        first_product(bank_a2[:], 1, slice(0, J))
+        first_product(bank_a1[:], 1, slice(0, HALF))
+        first_product(bank_a2[:, 0, :], 0, slice(HALF, J))
+        first_product(bank_a2[:, 1, :], 1, slice(HALF, J))
         first_product(bank_a3[:, 0, :], 2, slice(0, J))
         first_product(bank_a3[:, 1, :], 3, slice(0, J))
-        nc.scalar.copy(out=a_sb[:, 0, 0:HALF], in_=bank_a0[:])
-        nc.scalar.copy(out=a_sb[:, 0, HALF:J], in_=bank_a1[:])
-        nc.scalar.copy(out=a_sb[:, 1, :], in_=bank_a2[:])
-        nc.scalar.copy(out=a_sb[:, 2:4, :], in_=bank_a3[:])
+        nc.scalar.copy(out=a_all[:, 0, 0:HALF], in_=bank_a0[:])
+        nc.scalar.copy(out=a_all[:, 1, 0:HALF], in_=bank_a1[:])
+        nc.scalar.copy(out=a_all[:, 0:2, HALF:J], in_=bank_a2[:])
+        nc.scalar.copy(out=a_all[:, 2:4, :], in_=bank_a3[:])
 
-        xo_codes = sb_tile("xo_codes", [P, J], U16, tag="xc1")
+        xo_codes = sb_tile("xo_codes", [P, J], U16, tag="xc0")
         nc.vector.tensor_copy(out=xo_codes[:], in_=xo_all[:].indirect(l3[:]))
 
         for h in range(2):
-            nc.vector.tensor_copy(
-                out=board[0][:].indirect(l4[:, h * 8 : (h + 1) * 8]), in_=a_sb[:, 0, h * HALF : (h + 1) * HALF]
-            )
-        for t in range(1, PACK):
-            nc.vector.tensor_copy(out=board[t][:].indirect(l4[:]), in_=a_sb[:, t, :])
+            for t in range(2):
+                nc.vector.tensor_copy(
+                    out=board[t][:].indirect(l4[:, h * 8 : (h + 1) * 8]), in_=a_all[:, t, h * HALF : (h + 1) * HALF]
+                )
+        for t in range(2, PACK):
+            nc.vector.tensor_copy(out=board[t][:].indirect(l4[:]), in_=a_all[:, t, :])
 
-        w2_codes = sb_tile("w2_codes", [P, PACK, P], U32)
-        nc.scalar.copy(out=w2_codes[:], in_=dealt(w2_raw))
         bank_b = [psum.tile([P, 2, J], F32, name="bank_b%d" % u) for u in range(2)]
-        for t in range(PACK):
+        for h in range(2):
+            cols = slice(h * HALF, (h + 1) * HALF)
+            bank_bt = psum.tile([P, R], F32, name="bank_bt%d" % h, tag="bank_a%d" % h)
             nc.tensor.matmul_mx(
-                out=bank_b[t // 2][:, t % 2, :], lhsT=w2_codes[:, t, :].bitcast(FP8X4), lhsT_scale=w2_plane[:, t, :],
-                rhs=xo_codes[:].bitcast(FP4X4), rhs_scale=xo_plane[:], start=True, stop=True,
+                out=bank_bt[:], lhsT=xo_codes[:, cols].bitcast(FP4X4), lhsT_scale=xo_plane[:, cols],
+                rhs=w2_codes[:].bitcast(FP8X4), rhs_scale=w2_plane[:], start=True, stop=True,
             )
+            bt_sb = sb_tile("bt_sb%d" % h, [P, PACK, P], F32)
+            nc.scalar.copy(out=bt_sb[:], in_=dealt(bank_bt))
+            for t in range(PACK):
+                nc.tensor.transpose(bank_b[t // 2][:, t % 2, cols], bt_sb[:, t, :], identity[:])
 
         read = []
         for t in range(PACK):
-            read.append(sb_tile("read%d" % t, [P, J], F32, tag="w2_raw" if t == 0 else None))
+            read.append(sb_tile("read%d" % t, [P, J], F32, tag="bt_sb0" if t == 0 else None))
             nc.scalar.activation(out=read[t][:], in_=board[t][:].indirect(l5[:]), func=COPY, scale=sa_t[:, t : t + 1])
         answer = []
         for t in range(PACK):
-            answer.append(sb_tile("answer%d" % t, [P, J], F32))
+            answer.append(shared.tile([P, J], F32, name="answer%d" % t, offset=4 * J * t))
             nc.vector.tensor_tensor(out=answer[t][:], in0=read[t][:], in1=bank_b[t // 2][:, t % 2, :], op=MAX)
         hid_rows = sb_tile("hid_rows", [P, PACK, O], BF16)
         for t in range(PACK):
             nc.scalar.activation(out=hid_rows[:, t, :], in_=answer[t][:].indirect(l6[:]), func=COPY, scale=sb_t[:, t : t + 1])
 
-        xr_plane = sb_tile("xr_plane", [P, O], U8, tag="read3")
+        xr_plane = sb_tile("xr_plane", [P, O], U8, tag="read1")
         xr_codes = sb_tile("xr_codes", [P, O], U16, tag="read2")
         nc.vector.tensor_copy(out=xr_plane[:], in_=xr_plane_all[:].indirect(l7[:]))
         nc.vector.tensor_copy(out=xr_codes[:], in_=xr_all[:].indirect(l7[:]))

from contextlib import ExitStack

import concourse.mybir as mybir
from concourse.masks import make_identity

K, J, R, T, M, O, C, N, V = 512, 256, 512, 1024, 1024, 128, 512, 256, 1024
FLOPS = 2 * (K * R * J + 512 * R * J + R * N * O + 512 * N * O)

F32 = mybir.dt.float32
BF16 = mybir.dt.bfloat16
I32 = mybir.dt.int32
U32 = mybir.dt.uint32
U16 = mybir.dt.uint16
U8 = mybir.dt.uint8
FP8X4 = mybir.dt.float8_e4m3fn_x4
FP4X4 = mybir.dt.float4_e2m1fn_x4
COPY = mybir.ActivationFunctionType.Copy
MULT = mybir.AluOpType.mult
MAX = mybir.AluOpType.max

P = 128
PACK = 4
HALF = J // 2


def tile_picked_codegain_plain_two_answered_reminder_plain_kernel(
    tc, ta, tb, ga, gb, w_words, w_scales, xo_words, xo_scales, w2_words, w2_scales, sa, sb,
    wb_words, wb_scales, xr_words, xr_scales, ws_words, ws_scales,
    offs, offs2, offs3, offs4, offs5, offs6, offs7, out,
):
    nc = tc.nc
    with ExitStack() as ctx:
        keep = ctx.enter_context(tc.tile_pool(name="keep", bufs=1))
        shared = ctx.enter_context(tc.tile_pool(name="shared", bufs=1))
        psum = ctx.enter_context(tc.psum_pool(name="psum", bufs=1))

        def sb_tile(name, shape, dtype, tag=None):
            return keep.tile(shape, dtype, name=name, tag=tag or name, align_bytes=64)

        def load_list(name, src):
            lst = keep.tile(list(src.shape), U16, name=name)
            nc.sync.dma_start(lst[:], src)
            return lst

        def load_gain(name, src):
            gain = keep.tile([P, PACK], F32, name=name)
            nc.sync.dma_start(gain[:], src.rearrange("(p t) o -> p (t o)", t=PACK))
            return gain

        def load_rows(name, src, t):
            rows = sb_tile(name, [P, T], F32)
            nc.sync.dma_start(rows[:], src.rearrange("(p t) c -> p t c", t=PACK)[:, t, :])
            return rows

        def zeroed_plane(name, width):
            plane = sb_tile(name, [P, width], U8)
            nc.vector.memset(plane[:].bitcast(I32), 0)
            return plane

        def load_plane(plane, src):
            by_row = src[0].rearrange("(q r) n -> r q n", r=4)
            for r in range(4):
                nc.sync.dma_start(plane[r:P:32, :].bitcast(I32), by_row[r].bitcast(I32))

        def load_stage(name, src):
            stage = sb_tile(name, [P, 2, src.shape[2]], U8)
            by_row = src[0].rearrange("(q r) n -> r q n", r=4)
            for u in range(2):
                nc.sync.dma_start(
                    stage[64 * u : 64 * u + 4, :, :].bitcast(I32), by_row[:, 2 * u : 2 * u + 2, :].bitcast(I32)
                )
            return stage

        def spread_plane(plane, stage):
            for q in range(4):
                first = 64 * (q // 2)
                nc.vector.tensor_copy(
                    out=plane[32 * q : 32 * q + 4, :].bitcast(I32), in_=stage[first : first + 4, q % 2, :].bitcast(I32)
                )

        def load_fp4_words(name, src, width):
            words = sb_tile(name, [P, width], U16)
            nc.sync.dma_start(words[:].bitcast(I32), src[0].bitcast(I32))
            return words

        def load_fp8_words(name, src, width):
            words = sb_tile(name, [P, width], U32)
            nc.sync.dma_start(words[:].bitcast(I32), src[0].rearrange("p n t -> p (n t)").bitcast(I32))
            return words

        def dealt(src):
            return src[:].rearrange("p (m t) -> p t m", t=PACK)

        w_plane_raw = zeroed_plane("w_plane_raw", R)
        xo_plane_all = zeroed_plane("xo_plane_all", M)
        w2_plane = zeroed_plane("w2_plane", R)
        xr_plane_all = zeroed_plane("xr_plane_all", V)
        ws_plane = zeroed_plane("ws_plane", N)
        wb_plane = zeroed_plane("wb_plane", N)
        board = []
        for t in range(PACK):
            board.append(sb_tile("board%d" % t, [P, C], F32))
            nc.vector.memset(board[t][:], 0.0)

        identity = sb_tile("identity", [P, P], F32)
        make_identity(nc, identity[:])

        ta_rows, tb_rows = [], []
        ta_rows.append(load_rows("ta0", ta, 0))
        l1 = load_list("l1", offs)
        ga_t = load_gain("ga_t", ga)
        tb_rows.append(load_rows("tb0", tb, 0))
        l2 = load_list("l2", offs2)
        gb_t = load_gain("gb_t", gb)
        ta_rows.append(load_rows("ta1", ta, 1))
        xo_stage = load_stage("xo_stage", xo_scales)
        tb_rows.append(load_rows("tb1", tb, 1))
        w_stage = load_stage("w_stage", w_scales)
        ta_rows.append(load_rows("ta2", ta, 2))
        l3 = load_list("l3", offs3)
        tb_rows.append(load_rows("tb2", tb, 2))
        ta_rows.append(load_rows("ta3", ta, 3))
        tb_rows.append(load_rows("tb3", tb, 3))
        w_raw = load_fp4_words("w_raw", w_words, R)
        xo_all = load_fp4_words("xo_all", xo_words, M)
        l4 = load_list("l4", offs4)
        w2_codes = load_fp8_words("w2_codes", w2_words, R)
        load_plane(w2_plane, w2_scales)
        l5 = load_list("l5", offs5)
        sa_t = load_gain("sa_t", sa)
        l6 = load_list("l6", offs6)
        sb_t = load_gain("sb_t", sb)
        l7 = load_list("l7", offs7)
        load_plane(xr_plane_all, xr_scales)
        xr_all = load_fp4_words("xr_all", xr_words, V)
        ws_codes = load_fp8_words("ws_codes", ws_words, N)
        load_plane(ws_plane, ws_scales)
        wb_codes = load_fp8_words("wb_codes", wb_words, N)
        load_plane(wb_plane, wb_scales)

        spread_plane(xo_plane_all, xo_stage)
        spread_plane(w_plane_raw, w_stage)
        w_plane = sb_tile("w_plane", [P, PACK, P], U8)
        nc.vector.tensor_copy(out=w_plane[:], in_=dealt(w_plane_raw))
        xo_plane = sb_tile("xo_plane", [P, J], U8)
        nc.vector.tensor_copy(out=xo_plane[:], in_=xo_plane_all[:].indirect(l3[:]))

        xc = [sb_tile("xc%d" % h, [P, HALF, PACK], BF16) for h in range(2)]
        for t in range(PACK):
            step = sb_tile("step%d" % t, [P, J], F32)
            gain = sb_tile("gain%d" % t, [P, J], F32)
            nc.scalar.activation(out=step[:], in_=ta_rows[t][:].indirect(l1[:]), func=COPY, scale=ga_t[:, t : t + 1])
            nc.scalar.activation(out=gain[:], in_=tb_rows[t][:].indirect(l2[:]), func=COPY, scale=gb_t[:, t : t + 1])
            for h in range(2):
                cols = slice(h * HALF, (h + 1) * HALF)
                nc.vector.tensor_tensor(out=xc[h][:, :, t], in0=step[:, cols], in1=gain[:, cols], op=MULT)

        w_codes = sb_tile("w_codes", [P, PACK, P], U16)
        for t in range(PACK):
            nc.scalar.copy(out=w_codes[:, t, :], in_=dealt(w_raw)[:, t, :])

        xc_codes = sb_tile("xc_codes", [P, J], U32)
        xc_plane = sb_tile("xc_plane", [P, J], U8)
        for h in range(2):
            cols = slice(h * HALF, (h + 1) * HALF)
            nc.vector.quantize_mx(
                out=xc_codes[:, cols].bitcast(FP8X4), scales=xc_plane[:, cols],
                in_=xc[h][:].rearrange("p j t -> p (j t)"),
            )

        a_all = shared.tile([P, PACK, J], F32, name="a_all", offset=0)
        bank_a0 = psum.tile([P, HALF], F32, name="bank_a0")
        bank_a1 = psum.tile([P, HALF], F32, name="bank_a1")
        bank_a2 = psum.tile([P, 2, HALF], F32, name="bank_a2")
        bank_a3 = psum.tile([P, 2, J], F32, name="bank_a3")

        def first_product(dst, t, cols):
            nc.tensor.matmul_mx(
                out=dst, lhsT=w_codes[:, t, :].bitcast(FP4X4), lhsT_scale=w_plane[:, t, :],
                rhs=xc_codes[:, cols].bitcast(FP8X4), rhs_scale=xc_plane[:, cols], start=True, stop=True,
            )

        first_product(bank_a0[:], 0, slice(0, HALF))
        first_product(bank_a1[:], 1, slice(0, HALF))
        first_product(bank_a2[:, 0, :], 0, slice(HALF, J))
        first_product(bank_a2[:, 1, :], 1, slice(HALF, J))
        first_product(bank_a3[:, 0, :], 2, slice(0, J))
        first_product(bank_a3[:, 1, :], 3, slice(0, J))
        nc.scalar.copy(out=a_all[:, 0, 0:HALF], in_=bank_a0[:])
        nc.scalar.copy(out=a_all[:, 1, 0:HALF], in_=bank_a1[:])
        nc.scalar.copy(out=a_all[:, 0:2, HALF:J], in_=bank_a2[:])
        nc.scalar.copy(out=a_all[:, 2:4, :], in_=bank_a3[:])

        xo_codes = sb_tile("xo_codes", [P, J], U16, tag="xc0")
        nc.vector.tensor_copy(out=xo_codes[:], in_=xo_all[:].indirect(l3[:]))

        for h in range(2):
            for t in range(2):
                nc.vector.tensor_copy(
                    out=board[t][:].indirect(l4[:, h * 8 : (h + 1) * 8]), in_=a_all[:, t, h * HALF : (h + 1) * HALF]
                )
        for t in range(2, PACK):
            nc.vector.tensor_copy(out=board[t][:].indirect(l4[:]), in_=a_all[:, t, :])

        bank_b = [psum.tile([P, 2, J], F32, name="bank_b%d" % u) for u in range(2)]
        for h in range(2):
            cols = slice(h * HALF, (h + 1) * HALF)
            bank_bt = psum.tile([P, R], F32, name="bank_bt%d" % h, tag="bank_a%d" % h)
            nc.tensor.matmul_mx(
                out=bank_bt[:], lhsT=xo_codes[:, cols].bitcast(FP4X4), lhsT_scale=xo_plane[:, cols],
                rhs=w2_codes[:].bitcast(FP8X4), rhs_scale=w2_plane[:], start=True, stop=True,
            )
            bt_sb = sb_tile("bt_sb%d" % h, [P, PACK, P], F32)
            nc.scalar.copy(out=bt_sb[:], in_=dealt(bank_bt))
            for t in range(PACK):
                nc.tensor.transpose(bank_b[t // 2][:, t % 2, cols], bt_sb[:, t, :], identity[:])

        read = []
        for t in range(PACK):
            read.append(sb_tile("read%d" % t, [P, J], F32, tag="bt_sb0" if t == 0 else None))
            nc.scalar.activation(out=read[t][:], in_=board[t][:].indirect(l5[:]), func=COPY, scale=sa_t[:, t : t + 1])
        answer = []
        for t in range(PACK):
            answer.append(shared.tile([P, J], F32, name="answer%d" % t, offset=4 * J * t))
            nc.vector.tensor_tensor(out=answer[t][:], in0=read[t][:], in1=bank_b[t // 2][:, t % 2, :], op=MAX)
        hid_rows = sb_tile("hid_rows", [P, PACK, O], BF16)
        for t in range(PACK):
            nc.scalar.activation(out=hid_rows[:, t, :], in_=answer[t][:].indirect(l6[:]), func=COPY, scale=sb_t[:, t : t + 1])

        xr_plane = sb_tile("xr_plane", [P, O], U8, tag="read1")
        xr_codes = sb_tile("xr_codes", [P, O], U16, tag="read2")
        nc.vector.tensor_copy(out=xr_plane[:], in_=xr_plane_all[:].indirect(l7[:]))
        nc.vector.tensor_copy(out=xr_codes[:], in_=xr_all[:].indirect(l7[:]))
        bank_y = [psum.tile([P, O], F32, name="bank_y%d" % u) for u in range(2)]
        for u in range(2):
            cols = slice(u * P, (u + 1) * P)
            nc.tensor.matmul_mx(
                out=bank_y[u][:], lhsT=ws_codes[:, cols].bitcast(FP8X4), lhsT_scale=ws_plane[:, cols],
                rhs=xr_codes[:].bitcast(FP4X4), rhs_scale=xr_plane[:], start=True, stop=False,
            )

        hid = sb_tile("hid", [P, O, PACK], BF16, tag="xr_all")
        nc.vector.tensor_copy(out=hid[:], in_=hid_rows[:].rearrange("p t o -> p o t"))
        hid_codes = sb_tile("hid_codes", [P, O], U32)
        hid_plane = sb_tile("hid_plane", [P, O], U8)
        nc.vector.quantize_mx(
            out=hid_codes[:].bitcast(FP8X4), scales=hid_plane[:], in_=hid[:].rearrange("p o t -> p (o t)")
        )
        for u in range(2):
            cols = slice(u * P, (u + 1) * P)
            nc.tensor.matmul_mx(
                out=bank_y[u][:], lhsT=wb_codes[:, cols].bitcast(FP8X4), lhsT_scale=wb_plane[:, cols],
                rhs=hid_codes[:].bitcast(FP8X4), rhs_scale=hid_plane[:], start=False, stop=True,
            )
        y0 = sb_tile("y0", [P, O], F32)
        y1 = sb_tile("y1", [P, O], F32)
        nc.vector.tensor_copy(out=y0[:], in_=bank_y[0][:])
        nc.sync.dma_start(out[0:P, :], y0[:])
        nc.scalar.copy(out=y1[:], in_=bank_y[1][:])
        nc.scalar.dma_start(out[P:N, :], y1[:])
